import numpy as np
import ml_dtypes


def mxq(x, axis, fmt="e4m3"):
    dtype, down = {"e4m3": (ml_dtypes.float8_e4m3fn, 7), "e5m2": (ml_dtypes.float8_e5m2, 14)}[fmt]
    v = np.moveaxis(np.asarray(x, np.float32).astype(ml_dtypes.bfloat16).astype(np.float64), axis, -1)
    blocks = v.reshape(v.shape[:-1] + (-1, 32))
    amax = np.abs(blocks).max(-1, keepdims=True)
    byte = np.maximum(np.where(amax > 0, np.frexp(amax)[1] - 1 + 127, 0) - down, 1)
    scale = np.exp2(byte - 127.0)
    codes = (blocks / scale).astype(np.float32).astype(dtype).astype(np.float64)
    return np.moveaxis((codes * scale).reshape(v.shape), -1, axis)


WIDE = False


def mx_kscale(k):
    if not WIDE:
        return np.ones(k)
    levels = np.array([10, -10, 5, -5, 0])
    if k % 512:
        return np.exp2(np.random.permutation(np.resize(levels, k // 32))).repeat(32)
    a = np.empty((k // 512, 16))
    for p in range(k // 512):
        a[p, :8] = np.random.permutation(np.resize(levels, 8))
        for g in range(8):
            far = levels[np.abs(levels - a[p, g]) >= 10]
            a[p, g + 8] = far[np.random.randint(len(far))]
    return np.exp2(a.ravel()).repeat(32)


def f64(x):
    return np.asarray(x).astype(np.float64)


def striped(idx):
    return np.tile(np.asarray(idx).reshape(-1, 16).T, (8, 1)).astype(np.uint16)


def unstriped(offs):
    return offs[:16].T.reshape(-1).astype(np.int64)


E2M1 = np.array([0.0, 0.5, 1.0, 1.5, 2.0, 3.0, 4.0, 6.0, -0.0, -0.5, -1.0, -1.5, -2.0, -3.0, -4.0, -6.0])


def pack_weight(w, fmt):
    k, n = w.shape
    w = f64(np.asarray(w, np.float32).astype(ml_dtypes.bfloat16)).reshape(k // 32, 32, n)
    amax = np.abs(w).max(1)
    if fmt == "e4m3":
        byte = np.frexp(amax)[1] - 1 + 127 - 7
    else:
        mant, ex = np.frexp(amax / 6.0)
        byte = np.where(mant > 0.5, ex, ex - 1) + 127
    byte = np.clip(np.where(amax > 0, byte, 1), 1, 254)
    scaled = (w * np.exp2(127.0 - byte)[:, None, :]).reshape(k, n).astype(np.float32)
    by_word = np.ascontiguousarray(scaled.reshape(k // 512, 128, 4, n).transpose(0, 1, 3, 2))
    if fmt == "e4m3":
        words = by_word.astype(ml_dtypes.float8_e4m3fn).view(np.uint8)
    else:
        c = by_word.astype(ml_dtypes.float4_e2m1fn).view(np.uint8) & 0xF
        words = (c[..., 0::2] | (c[..., 1::2] << 4)).reshape(k // 512, 128, 2 * n)
    return np.ascontiguousarray(words), np.ascontiguousarray(byte.astype(np.uint8).reshape(k // 512, 16, n))


def unpack_weight(words, scales, fmt):
    g, _, n = scales.shape
    words = np.ascontiguousarray(words).reshape(g, 128, n, -1)
    if fmt == "e4m3":
        vals = words.view(ml_dtypes.float8_e4m3fn).astype(np.float64)
    else:
        nib = np.empty((g, 128, n, 4), np.uint8)
        nib[..., 0::2] = words & 0xF
        nib[..., 1::2] = words >> 4
        vals = E2M1[nib]
    vals = vals * np.repeat(np.exp2(scales.astype(np.float64) - 127.0), 8, axis=1)[..., None]
    return vals.transpose(0, 1, 3, 2).reshape(g * 512, n)


D, E, T, I, G, U, Q = 512, 512, 4096, 1024, 64, 512, 128


def setup_inputs():
    n = np.random.standard_normal
    idx = np.random.permutation(T)[:I]
    idx2 = np.random.permutation(U)[:G]
    fd = mx_kscale(D)
    fe = mx_kscale(E)
    keysp = pack_weight(n((D, T)) / fd[:, None], "e4m3")
    valsp = pack_weight(n((E, T)) / fe[:, None], "e4m3")
    return {
        "query": (n((D, Q)) * 0.6 / np.sqrt(D) * fd[:, None]).astype(np.float32),
        "keys_words": keysp[0],
        "keys_scales": keysp[1],
        "ptab": (0.5 * n((Q, U)) - 0.4).astype(np.float32),
        "age": (np.random.uniform(0.0, 2.0, (1, I))).astype(np.float32),
        "gout": (n((E, Q)) * 1 / np.sqrt(E) * fe[:, None]).astype(np.float32),
        "vals_words": valsp[0],
        "vals_scales": valsp[1],
        "old": (0.5 * n((Q, U))).astype(np.float32),
        "offs": striped(idx),
        "offs2": striped(idx2),
    }


def reference(query, keys_words, keys_scales, ptab, age, gout, vals_words, vals_scales, old, offs, offs2):
    idx = unstriped(offs)
    idx2 = unstriped(offs2)
    keysu = unpack_weight(keys_words, keys_scales, "e4m3")
    valsu = unpack_weight(vals_words, vals_scales, "e4m3")
    queryq = mxq(f64(query), 0, "e4m3")
    keysidxg = keysu[:, idx]
    a = queryq.T @ keysidxg
    tp = np.exp(f64(ptab)[:, idx2])
    tr1 = np.repeat(tp, I // G, axis=1)
    p = np.exp(a - f64(age) * tr1)
    z = np.sum(p, axis=1, keepdims=True)
    goutq = mxq(f64(gout), 0, "e4m3")
    valsidxg = valsu[:, idx]
    c0 = goutq.T @ valsidxg
    dz = np.sum(p * c0, axis=1, keepdims=True) / np.square(z) * (-1.0)
    dp = 1.0 / z * c0 + dz
    dtr1 = dp * p * (-1.0) * f64(age)
    dtp = dtr1.reshape(Q, G, I // G).sum(axis=2)
    gs = dtp * tp * 64.0
    gf = np.zeros((Q, U))
    gf[:, idx2] = gs
    y = f64(old) + gf
    return y

@@ -1,0 +1,186 @@
+import math
+from contextlib import ExitStack
+
+import concourse.mybir as mybir
+from concourse.masks import make_identity
+
+D, E, T, I, G, U, Q = 512, 512, 4096, 1024, 64, 512, 128
+FLOPS = 2 * Q * I * (D + E)
+
+F32 = mybir.dt.float32
+BF16 = mybir.dt.bfloat16
+I32 = mybir.dt.int32
+U32 = mybir.dt.uint32
+U16 = mybir.dt.uint16
+U8 = mybir.dt.uint8
+FP8X4 = mybir.dt.float8_e4m3fn_x4
+ALU = mybir.AluOpType
+ACT = mybir.ActivationFunctionType
+AX = mybir.AxisListType
+
+P = 128
+PACK = 4
+HALF = 512
+HALVES = I // HALF
+PAGE = I // G
+SOFT = 8.0
+VAL_PLANE = 4
+
+
+def tile_attend_bpagerate_kernel(tc, query, keys_words, keys_scales, ptab, age, gout,
+                                  vals_words, vals_scales, old, offs, offs2, out):
+    nc = tc.nc
+    with ExitStack() as ctx:
+        lists = ctx.enter_context(tc.tile_pool(name="lists", bufs=1))
+        sb = ctx.enter_context(tc.tile_pool(name="sb", bufs=1))
+        ps = ctx.enter_context(tc.psum_pool(name="ps", bufs=1))
+
+        slots = lists.tile([P, I // 16], U16, name="slots")
+        pages = lists.tile([P, G // 16], U16, name="pages")
+        nc.sync.dma_start(slots[:], offs)
+        nc.sync.dma_start(pages[:], offs2)
+
+        def half_list(h):
+            return slots[:, h * (HALF // 16):(h + 1) * (HALF // 16)]
+
+        age_col = sb.tile([P, HALVES, PACK], F32, name="age_col")
+        nc.sync.dma_start(age_col[:], age[0].rearrange("(h p c) -> p h c", h=HALVES, c=PACK))
+        key_scales = sb.tile([P, T], U8, name="key_scales")
+        val_scales = sb.tile([P, T], U8, name="val_scales")
+        nc.gpsimd.memset(key_scales[:].bitcast(I32)[:, :T // 8], 0)
+        nc.vector.memset(key_scales[:].bitcast(I32)[:, T // 8:], 0)
+        nc.vector.memset(val_scales[:].bitcast(I32), 0)
+
+        ptab_sb = sb.tile([P, U], F32, name="ptab_sb", tag="stage")
+        nc.sync.dma_start(ptab_sb[:], ptab)
+        query_sb = sb.tile([P, PACK, Q], F32, name="query_sb", tag="rows")
+        nc.sync.dma_start(query_sb[:], query.rearrange("(p j) q -> p j q", j=PACK))
+        for quad in range(4):
+            nc.sync.dma_start(key_scales[:].bitcast(I32)[32 * quad:32 * quad + 4, :],
+                              keys_scales[0, 4 * quad:4 * quad + 4, :].bitcast(I32))
+        key_words = sb.tile([P, T], U32, name="key_words")
+        nc.sync.dma_start(key_words[:].bitcast(I32),
+                          keys_words[0].rearrange("p t r -> p (t r)").bitcast(I32))
+
+        ident = sb.tile([P, P], F32, name="ident")
+        make_identity(nc, ident[:])
+        for quad in range(4):
+            first = 32 * quad + VAL_PLANE
+            nc.gpsimd.dma_start(val_scales[:].bitcast(I32)[first:first + 4, :],
+                                vals_scales[0, 4 * quad:4 * quad + 4, :].bitcast(I32))
+        placed = sb.tile([P, U], F32, name="placed")
+        nc.gpsimd.memset(placed[:], 0.0)
+        factor = sb.tile([P, G], F32, name="factor")
+        nc.gpsimd.memset(factor[:], -64.0)
+
+        log_rate = sb.tile([P, G], F32, name="log_rate", tag="vals")
+        nc.vector.tensor_copy(log_rate[:], ptab_sb[:].indirect(pages[:]))
+        rate = sb.tile([P, G], F32, name="rate")
+        nc.scalar.activation(rate[:], log_rate[:], ACT.Exp)
+
+        val_words = sb.tile([P, T], U32, name="val_words", tag="vals")
+        nc.sync.dma_start(val_words[:].bitcast(I32),
+                          vals_words[0].rearrange("p t r -> p (t r)").bitcast(I32))
+
+        age_rows = [ps.tile([P, PACK, P], F32, name=f"age_rows{h}") for h in range(HALVES)]
+        for h in range(HALVES):
+            for c in range(PACK):
+                nc.tensor.transpose(age_rows[h][:, c, :], age_col[:, h, c:c + 1].to_broadcast([P, P]), ident[:])
+
+        def gather(name, window, dtype, h, tag):
+            picked = sb.tile([P, HALF], dtype, name=f"{name}{h}", tag=tag, align_bytes=64)
+            nc.vector.tensor_copy(picked[:], window[:].indirect(half_list(h)))
+            return picked
+
+        def interleave(name, raw):
+            grouped = sb.tile([P, Q, PACK], BF16, name=f"{name}_grouped", align_bytes=64)
+            nc.scalar.copy(grouped[:], raw[:].rearrange("p j q -> p q j"))
+            return grouped
+
+        def quantize(name, grouped):
+            codes = sb.tile([P, Q], U32, name=f"{name}_codes", align_bytes=64)
+            scales = sb.tile([P, Q], U8, name=f"{name}_scales", align_bytes=64)
+            nc.vector.quantize_mx(out=codes[:].bitcast(FP8X4), scales=scales[:],
+                                  in_=grouped[:].rearrange("p q j -> p (q j)"))
+            return codes, scales
+
+        def product(name, rows, words, scales, h):
+            bank = ps.tile([P, HALF], F32, name=f"{name}{h}")
+            nc.tensor.matmul_mx(out=bank[:], lhsT=rows[0][:].bitcast(FP8X4), lhsT_scale=rows[1][:],
+                                rhs=words[:].bitcast(FP8X4), rhs_scale=scales,
+                                start=True, stop=True)
+            return bank
+
+        ks = [gather("ks", key_scales, U8, h, f"ks{h}") for h in range(HALVES)]
+        fade = sb.tile([P, I], F32, name="fade")
+        for h in range(HALVES):
+            half_pages = G // HALVES
+            nc.vector.tensor_tensor(
+                fade[:, h * HALF:(h + 1) * HALF].rearrange("q (g r c) -> q g r c", r=PACK, c=PACK),
+                age_rows[h][:].rearrange("q c (g r) -> q g r c", r=PACK),
+                rate[:, h * half_pages:(h + 1) * half_pages].unsqueeze(2).unsqueeze(3).to_broadcast(
+                    [P, half_pages, PACK, PACK]),
+                ALU.mult)
+        query_grouped = interleave("query", query_sb)
+        kw0 = gather("kw", key_words, U32, 0, "kw0")
+        query_mx = quantize("query", query_grouped)
+        kw = [kw0, gather("kw", key_words, U32, 1, "kw1")]
+        score = [product("score", query_mx, kw[h], ks[h][:], h) for h in range(HALVES)]
+
+        gout_sb = sb.tile([P, PACK, Q], F32, name="gout_sb", tag="rows")
+        nc.sync.dma_start(gout_sb[:], gout.rearrange("(p j) q -> p j q", j=PACK))
+
+        logit = sb.tile([P, I], F32, name="logit")
+        weight = sb.tile([P, I], F32, name="weight")
+        soft_sums = sb.tile([P, HALVES], F32, name="soft_sums")
+        for h in range(HALVES):
+            cols = slice(h * HALF, (h + 1) * HALF)
+            nc.vector.tensor_tensor(logit[:, cols], score[h][:], fade[:, cols], ALU.subtract)
+            nc.scalar.activation(weight[:, cols], logit[:, cols], ACT.Exp, scale=1.0 / SOFT,
+                                 accum_out=soft_sums[:, h:h + 1])
+        vs = [gather("vs", val_scales, U8, h, "ks1" if h == 0 else "kw1") for h in range(HALVES)]
+        soft_sum = sb.tile([P, 1], F32, name="soft_sum")
+        nc.scalar.activation(soft_sum[:], soft_sums[:, 0:1], ACT.Identity, bias=soft_sums[:, 1:2])
+        shift = sb.tile([P, 1], F32, name="shift")
+        nc.scalar.activation(shift[:], soft_sum[:].bitcast(U32), ACT.Copy,
+                             scale=-SOFT * math.log(2.0) / 2.0 ** 23,
+                             bias=SOFT * (127.0 * math.log(2.0) + 0.5 * math.log(I)))
+        total = sb.tile([P, 1], F32, name="total")
+        nc.scalar.activation(weight[:], logit[:], ACT.Exp, bias=shift[:], accum_out=total[:])
+        gout_grouped = interleave("gout", gout_sb)
+        old_sb = sb.tile([P, U], F32, name="old_sb", tag="rows")
+        nc.sync.dma_start(old_sb[:], old)
+
+        inv_total = sb.tile([P, 1], F32, name="inv_total")
+        nc.vector.reciprocal(inv_total[:], total[:])
+        faded = sb.tile([P, I], F32, name="faded")
+        nc.vector.scalar_tensor_tensor(faded[:], weight[:], inv_total[:], fade[:], ALU.mult, ALU.mult)
+
+        vw0 = gather("vw", val_words, U32, 0, "vw0")
+        gout_mx = quantize("gout", gout_grouped)
+        vw = [vw0, gather("vw", val_words, U32, 1, "vw1")]
+        pull = [product("pull", gout_mx, vw[h], vs[h][VAL_PLANE:P, :], h) for h in range(HALVES)]
+
+        terms = sb.tile([P, I], F32, name="terms")
+        means = sb.tile([P, HALVES], F32, name="means")
+        for h in range(HALVES):
+            cols = slice(h * HALF, (h + 1) * HALF)
+            nc.vector.scalar_tensor_tensor(logit[:, cols], pull[h][:], inv_total[:], weight[:, cols],
+                                           ALU.mult, ALU.mult, accum_out=means[:, h:h + 1])
+        mean = sb.tile([P, 1], F32, name="mean")
+        nc.vector.tensor_tensor(mean[:], means[:, 0:1], means[:, 1:2], ALU.add)
+        for h in range(HALVES):
+            cols = slice(h * HALF, (h + 1) * HALF)
+            nc.vector.scalar_tensor_tensor(terms[:, cols], pull[h][:], mean[:], faded[:, cols],
+                                           ALU.subtract, ALU.mult)
+        page_sums = sb.tile([P, G], F32, name="page_sums")
+        for h in range(HALVES):
+            nc.vector.tensor_reduce(page_sums[:, h * G // 2:(h + 1) * G // 2],
+                                    terms[:, h * HALF:(h + 1) * HALF].rearrange("q (g r) -> q g r", r=PAGE),
+                                    AX.X, ALU.add)
+        nc.vector.tensor_tensor(placed[:].indirect(pages[:]), page_sums[:], factor[:], ALU.mult)
+        result = sb.tile([P, U], F32, name="result")
+        for h in range(2):
+            cols = slice(h * U // 2, (h + 1) * U // 2)
+            nc.vector.tensor_tensor(result[:, cols], placed[:, cols], old_sb[:, cols], ALU.add)
+            nc.sync.dma_start(out[:, cols], result[:, cols])

@@ -24,7 +24,9 @@ HALF = 512
 HALVES = I // HALF
 PAGE = I // G
 SOFT = 8.0
-VAL_PLANE = 4
+BLOCK_ROWS = 8
+DEAL = I // P
+BANK_BLOCKS = HALF // P
 
 
 def tile_attend_bpagerate_kernel(tc, query, keys_words, keys_scales, ptab, age, gout,
@@ -37,55 +39,62 @@ def tile_attend_bpagerate_kernel(tc, query, keys_words, keys_scales, ptab, age, 
 
         slots = lists.tile([P, I // 16], U16, name="slots")
         pages = lists.tile([P, G // 16], U16, name="pages")
-        nc.sync.dma_start(slots[:], offs)
-        nc.sync.dma_start(pages[:], offs2)
 
         def half_list(h):
             return slots[:, h * (HALF // 16):(h + 1) * (HALF // 16)]
 
-        age_col = sb.tile([P, HALVES, PACK], F32, name="age_col")
-        nc.sync.dma_start(age_col[:], age[0].rearrange("(h p c) -> p h c", h=HALVES, c=PACK))
-        key_scales = sb.tile([P, T], U8, name="key_scales")
+        age_col = sb.tile([P, DEAL], F32, name="age_col")
+        nc.gpsimd.dma_start(age_col[:], age[0].rearrange("(p c) -> p c", c=DEAL))
+        key_scales = sb.tile([P, T], U8, name="key_scales", tag="vals")
         val_scales = sb.tile([P, T], U8, name="val_scales")
-        nc.gpsimd.memset(key_scales[:].bitcast(I32)[:, :T // 8], 0)
-        nc.vector.memset(key_scales[:].bitcast(I32)[:, T // 8:], 0)
+        nc.vector.memset(key_scales[:].bitcast(I32), 0)
         nc.vector.memset(val_scales[:].bitcast(I32), 0)
 
-        ptab_sb = sb.tile([P, U], F32, name="ptab_sb", tag="stage")
+        nc.sync.dma_start(slots[:], offs)
+        nc.sync.dma_start(pages[:], offs2)
+        ptab_sb = sb.tile([P, U], F32, name="ptab_sb")
         nc.sync.dma_start(ptab_sb[:], ptab)
-        query_sb = sb.tile([P, PACK, Q], F32, name="query_sb", tag="rows")
+        query_sb = sb.tile([P, PACK, Q], F32, name="query_sb")
         nc.sync.dma_start(query_sb[:], query.rearrange("(p j) q -> p j q", j=PACK))
-        for quad in range(4):
-            nc.sync.dma_start(key_scales[:].bitcast(I32)[32 * quad:32 * quad + 4, :],
-                              keys_scales[0, 4 * quad:4 * quad + 4, :].bitcast(I32))
+        nc.sync.dma_start(key_scales[:].bitcast(I32)[0:P:BLOCK_ROWS, :], keys_scales[0].bitcast(I32))
+        nc.sync.dma_start(val_scales[:].bitcast(I32)[0:P:BLOCK_ROWS, :], vals_scales[0].bitcast(I32))
         key_words = sb.tile([P, T], U32, name="key_words")
         nc.sync.dma_start(key_words[:].bitcast(I32),
                           keys_words[0].rearrange("p t r -> p (t r)").bitcast(I32))
+        gout_sb = sb.tile([P, PACK, Q], F32, name="gout_sb", tag="rows")
+        nc.sync.dma_start(gout_sb[:], gout.rearrange("(p j) q -> p j q", j=PACK))
 
         ident = sb.tile([P, P], F32, name="ident")
         make_identity(nc, ident[:])
-        for quad in range(4):
-            first = 32 * quad + VAL_PLANE
-            nc.gpsimd.dma_start(val_scales[:].bitcast(I32)[first:first + 4, :],
-                                vals_scales[0, 4 * quad:4 * quad + 4, :].bitcast(I32))
         placed = sb.tile([P, U], F32, name="placed")
         nc.gpsimd.memset(placed[:], 0.0)
-        factor = sb.tile([P, G], F32, name="factor")
-        nc.gpsimd.memset(factor[:], -64.0)
 
-        log_rate = sb.tile([P, G], F32, name="log_rate", tag="vals")
+        log_rate = sb.tile([P, G], F32, name="log_rate")
         nc.vector.tensor_copy(log_rate[:], ptab_sb[:].indirect(pages[:]))
-        rate = sb.tile([P, G], F32, name="rate")
-        nc.scalar.activation(rate[:], log_rate[:], ACT.Exp)
+        rate = sb.tile([P, G, P // G], F32, name="rate")
+        nc.scalar.activation(rate[:], log_rate[:].unsqueeze(2).to_broadcast([P, G, P // G]), ACT.Exp)
+        rate_t = ps.tile([P, Q], F32, name="rate_t")
+        nc.tensor.transpose(rate_t[:], rate[:].rearrange("q g r -> q (g r)"), ident[:])
+        fade_t = sb.tile([P, DEAL, Q], F32, name="fade_t")
+        for c in range(DEAL):
+            nc.scalar.activation(fade_t[:, c, :], rate_t[:], ACT.Copy, scale=age_col[:, c:c + 1])
+        fade = sb.tile([P, I], F32, name="fade")
+        for b in range(HALVES):
+            turned = ps.tile([P, BANK_BLOCKS, P], F32, name=f"turned{b}")
+            for c in range(BANK_BLOCKS):
+                nc.tensor.transpose(turned[:, c, :], fade_t[:, b * BANK_BLOCKS + c, :], ident[:])
+            nc.scalar.copy(
+                fade[:].rearrange("q (p c) -> q p c", c=DEAL)[:, :, b * BANK_BLOCKS:(b + 1) * BANK_BLOCKS],
+                turned[:].rearrange("q c p -> q p c"))
 
-        val_words = sb.tile([P, T], U32, name="val_words", tag="vals")
-        nc.sync.dma_start(val_words[:].bitcast(I32),
-                          vals_words[0].rearrange("p t r -> p (t r)").bitcast(I32))
-
-        age_rows = [ps.tile([P, PACK, P], F32, name=f"age_rows{h}") for h in range(HALVES)]
-        for h in range(HALVES):
-            for c in range(PACK):
-                nc.tensor.transpose(age_rows[h][:, c, :], age_col[:, h, c:c + 1].to_broadcast([P, P]), ident[:])
+        def gather_plane(name, window):
+            picked = sb.tile([P, I], U8, name=f"{name}_picked")
+            nc.vector.tensor_copy(picked[:], window[:].indirect(slots[:]))
+            plane = sb.tile([P, I], U8, name=f"{name}_plane", align_bytes=64)
+            for r in range(4):
+                nc.sync.dma_start(plane[:].bitcast(I32)[r:P:32, :],
+                                  picked[:].bitcast(I32)[BLOCK_ROWS * r:P:32, :])
+            return plane
 
         def gather(name, window, dtype, h, tag):
             picked = sb.tile([P, HALF], dtype, name=f"{name}{h}", tag=tag, align_bytes=64)
@@ -105,30 +114,25 @@ def tile_attend_bpagerate_kernel(tc, query, keys_words, keys_scales, ptab, age, 
             return codes, scales
 
         def product(name, rows, words, scales, h):
-            bank = ps.tile([P, HALF], F32, name=f"{name}{h}")
+            bank = ps.tile([P, HALF], F32, name=f"{name}{h}", tag=f"{name}{h}")
             nc.tensor.matmul_mx(out=bank[:], lhsT=rows[0][:].bitcast(FP8X4), lhsT_scale=rows[1][:],
                                 rhs=words[:].bitcast(FP8X4), rhs_scale=scales,
                                 start=True, stop=True)
             return bank
 
-        ks = [gather("ks", key_scales, U8, h, f"ks{h}") for h in range(HALVES)]
-        fade = sb.tile([P, I], F32, name="fade")
-        for h in range(HALVES):
-            half_pages = G // HALVES
-            nc.vector.tensor_tensor(
-                fade[:, h * HALF:(h + 1) * HALF].rearrange("q (g r c) -> q g r c", r=PACK, c=PACK),
-                age_rows[h][:].rearrange("q c (g r) -> q g r c", r=PACK),
-                rate[:, h * half_pages:(h + 1) * half_pages].unsqueeze(2).unsqueeze(3).to_broadcast(
-                    [P, half_pages, PACK, PACK]),
-                ALU.mult)
+        key_plane = gather_plane("key", key_scales)
+        val_words = sb.tile([P, T], U32, name="val_words", tag="vals")
+        nc.sync.dma_start(val_words[:].bitcast(I32),
+                          vals_words[0].rearrange("p t r -> p (t r)").bitcast(I32))
         query_grouped = interleave("query", query_sb)
-        kw0 = gather("kw", key_words, U32, 0, "kw0")
         query_mx = quantize("query", query_grouped)
-        kw = [kw0, gather("kw", key_words, U32, 1, "kw1")]
-        score = [product("score", query_mx, kw[h], ks[h][:], h) for h in range(HALVES)]
-
-        gout_sb = sb.tile([P, PACK, Q], F32, name="gout_sb", tag="rows")
-        nc.sync.dma_start(gout_sb[:], gout.rearrange("(p j) q -> p j q", j=PACK))
+        val_plane = gather_plane("val", val_scales)
+        gout_grouped = interleave("gout", gout_sb)
+        old_sb = sb.tile([P, U], F32, name="old_sb", tag="rows")
+        nc.sync.dma_start(old_sb[:], old)
+        kw = [gather("kw", key_words, U32, h, f"kw{h}") for h in range(HALVES)]
+        score = [product("score", query_mx, kw[h], key_plane[:, h * HALF:(h + 1) * HALF], h) for h in range(HALVES)]
+        gout_mx = quantize("gout", gout_grouped)
 
         logit = sb.tile([P, I], F32, name="logit")
         weight = sb.tile([P, I], F32, name="weight")
@@ -138,7 +142,6 @@ def tile_attend_bpagerate_kernel(tc, query, keys_words, keys_scales, ptab, age, 
             nc.vector.tensor_tensor(logit[:, cols], score[h][:], fade[:, cols], ALU.subtract)
             nc.scalar.activation(weight[:, cols], logit[:, cols], ACT.Exp, scale=1.0 / SOFT,
                                  accum_out=soft_sums[:, h:h + 1])
-        vs = [gather("vs", val_scales, U8, h, "ks1" if h == 0 else "kw1") for h in range(HALVES)]
         soft_sum = sb.tile([P, 1], F32, name="soft_sum")
         nc.scalar.activation(soft_sum[:], soft_sums[:, 0:1], ACT.Identity, bias=soft_sums[:, 1:2])
         shift = sb.tile([P, 1], F32, name="shift")
@@ -147,25 +150,23 @@ def tile_attend_bpagerate_kernel(tc, query, keys_words, keys_scales, ptab, age, 
                              bias=SOFT * (127.0 * math.log(2.0) + 0.5 * math.log(I)))
         total = sb.tile([P, 1], F32, name="total")
         nc.scalar.activation(weight[:], logit[:], ACT.Exp, bias=shift[:], accum_out=total[:])
-        gout_grouped = interleave("gout", gout_sb)
-        old_sb = sb.tile([P, U], F32, name="old_sb", tag="rows")
-        nc.sync.dma_start(old_sb[:], old)
 
-        inv_total = sb.tile([P, 1], F32, name="inv_total")
-        nc.vector.reciprocal(inv_total[:], total[:])
-        faded = sb.tile([P, I], F32, name="faded")
-        nc.vector.scalar_tensor_tensor(faded[:], weight[:], inv_total[:], fade[:], ALU.mult, ALU.mult)
+        vw = [gather("vw", val_words, U32, h, f"vw{h}") for h in range(HALVES)]
+        pull = [product("pull", gout_mx, vw[h], val_plane[:, h * HALF:(h + 1) * HALF], h) for h in range(HALVES)]
 
-        vw0 = gather("vw", val_words, U32, 0, "vw0")
-        gout_mx = quantize("gout", gout_grouped)
-        vw = [vw0, gather("vw", val_words, U32, 1, "vw1")]
-        pull = [product("pull", gout_mx, vw[h], vs[h][VAL_PLANE:P, :], h) for h in range(HALVES)]
-
+        late = sb.tile([P, I + 1], F32, name="late", tag="vals")
+        faded, inv_total = late[:, :I], late[:, I:]
+        nc.vector.reciprocal(inv_total, total[:])
+        for h in range(HALVES):
+            cols = slice(h * HALF, (h + 1) * HALF)
+            nc.gpsimd.tensor_tensor(faded[:, cols], weight[:, cols], fade[:, cols], ALU.mult)
+        factor = sb.tile([P, G], F32, name="factor")
+        nc.scalar.activation(factor[:], inv_total.to_broadcast([P, G]), ACT.Copy, scale=-64.0)
         terms = sb.tile([P, I], F32, name="terms")
         means = sb.tile([P, HALVES], F32, name="means")
         for h in range(HALVES):
             cols = slice(h * HALF, (h + 1) * HALF)
-            nc.vector.scalar_tensor_tensor(logit[:, cols], pull[h][:], inv_total[:], weight[:, cols],
+            nc.vector.scalar_tensor_tensor(logit[:, cols], pull[h][:], inv_total, weight[:, cols],
                                            ALU.mult, ALU.mult, accum_out=means[:, h:h + 1])
         mean = sb.tile([P, 1], F32, name="mean")
         nc.vector.tensor_tensor(mean[:], means[:, 0:1], means[:, 1:2], ALU.add)

@@ -24,7 +24,10 @@ HALF = 512
 HALVES = I // HALF
 PAGE = I // G
 SOFT = 8.0
-BLOCK_ROWS = 8
+QUADRANT = 32
+SCALE_ROWS = 16
+COPIES = QUADRANT // SCALE_ROWS
+LAST_QUADRANT = P - QUADRANT
 DEAL = I // P
 BANK_BLOCKS = HALF // P
 
@@ -45,19 +48,22 @@ def tile_attend_bpagerate_kernel(tc, query, keys_words, keys_scales, ptab, age, 
 
         age_col = sb.tile([P, DEAL], F32, name="age_col")
         nc.gpsimd.dma_start(age_col[:], age[0].rearrange("(p c) -> p c", c=DEAL))
-        key_scales = sb.tile([P, T], U8, name="key_scales", tag="vals")
-        val_scales = sb.tile([P, T], U8, name="val_scales")
-        nc.vector.memset(key_scales[:].bitcast(I32), 0)
-        nc.vector.memset(val_scales[:].bitcast(I32), 0)
+        def scale_window(name, scales):
+            window = sb.tile([P, T], U8, name=name, tag=name)
+            words = window[:].bitcast(I32)
+            nc.vector.memset(words[:LAST_QUADRANT, :], 0)
+            nc.sync.dma_start(words[LAST_QUADRANT:, :],
+                              scales[0].bitcast(I32).unsqueeze(1).to_broadcast([SCALE_ROWS, COPIES, T // 4]))
+            return window
 
         nc.sync.dma_start(slots[:], offs)
+        key_scales = scale_window("vals", keys_scales)
         nc.sync.dma_start(pages[:], offs2)
         ptab_sb = sb.tile([P, U], F32, name="ptab_sb")
         nc.sync.dma_start(ptab_sb[:], ptab)
+        val_scales = scale_window("val_scales", vals_scales)
         query_sb = sb.tile([P, PACK, Q], F32, name="query_sb")
         nc.sync.dma_start(query_sb[:], query.rearrange("(p j) q -> p j q", j=PACK))
-        nc.sync.dma_start(key_scales[:].bitcast(I32)[0:P:BLOCK_ROWS, :], keys_scales[0].bitcast(I32))
-        nc.sync.dma_start(val_scales[:].bitcast(I32)[0:P:BLOCK_ROWS, :], vals_scales[0].bitcast(I32))
         key_words = sb.tile([P, T], U32, name="key_words")
         nc.sync.dma_start(key_words[:].bitcast(I32),
                           keys_words[0].rearrange("p t r -> p (t r)").bitcast(I32))
@@ -93,7 +99,7 @@ def tile_attend_bpagerate_kernel(tc, query, keys_words, keys_scales, ptab, age, 
             plane = sb.tile([P, I], U8, name=f"{name}_plane", align_bytes=64)
             for r in range(4):
                 nc.sync.dma_start(plane[:].bitcast(I32)[r:P:32, :],
-                                  picked[:].bitcast(I32)[BLOCK_ROWS * r:P:32, :])
+                                  picked[:].bitcast(I32)[LAST_QUADRANT + COPIES * r:P:4 * COPIES, :])
             return plane
 
         def gather(name, window, dtype, h, tag):
@@ -156,29 +162,30 @@ def tile_attend_bpagerate_kernel(tc, query, keys_words, keys_scales, ptab, age, 
 
         late = sb.tile([P, I + 1], F32, name="late", tag="vals")
         faded, inv_total = late[:, :I], late[:, I:]
-        nc.vector.reciprocal(inv_total, total[:])
         for h in range(HALVES):
             cols = slice(h * HALF, (h + 1) * HALF)
             nc.gpsimd.tensor_tensor(faded[:, cols], weight[:, cols], fade[:, cols], ALU.mult)
-        factor = sb.tile([P, G], F32, name="factor")
-        nc.scalar.activation(factor[:], inv_total.to_broadcast([P, G]), ACT.Copy, scale=-64.0)
         terms = sb.tile([P, I], F32, name="terms")
         means = sb.tile([P, HALVES], F32, name="means")
         for h in range(HALVES):
             cols = slice(h * HALF, (h + 1) * HALF)
-            nc.vector.scalar_tensor_tensor(logit[:, cols], pull[h][:], inv_total, weight[:, cols],
+            nc.vector.scalar_tensor_tensor(logit[:, cols], pull[h][:], 1.0, weight[:, cols],
                                            ALU.mult, ALU.mult, accum_out=means[:, h:h + 1])
         mean = sb.tile([P, 1], F32, name="mean")
-        nc.vector.tensor_tensor(mean[:], means[:, 0:1], means[:, 1:2], ALU.add)
+        nc.vector.reciprocal(inv_total, total[:])
+        nc.vector.tensor_scalar(mean[:], means[:, 0:1], means[:, 1:2], inv_total, ALU.add, ALU.mult)
+        factor = sb.tile([P, G], F32, name="factor")
+        nc.scalar.activation(factor[:], inv_total.to_broadcast([P, G]), ACT.Copy, scale=-64.0)
         for h in range(HALVES):
             cols = slice(h * HALF, (h + 1) * HALF)
             nc.vector.scalar_tensor_tensor(terms[:, cols], pull[h][:], mean[:], faded[:, cols],
                                            ALU.subtract, ALU.mult)
         page_sums = sb.tile([P, G], F32, name="page_sums")
-        for h in range(HALVES):
-            nc.vector.tensor_reduce(page_sums[:, h * G // 2:(h + 1) * G // 2],
-                                    terms[:, h * HALF:(h + 1) * HALF].rearrange("q (g r) -> q g r", r=PAGE),
-                                    AX.X, ALU.add)
+        by_page = terms[:].rearrange("q (g r) -> q g r", r=PAGE)
+        folded = sb.tile([P, G // 2, PAGE // 2], F32, name="folded")
+        nc.gpsimd.tensor_tensor(folded[:], by_page[:, :G // 2, :PAGE // 2], by_page[:, :G // 2, PAGE // 2:], ALU.add)
+        nc.vector.tensor_reduce(page_sums[:, G // 2:], by_page[:, G // 2:, :], AX.X, ALU.add)
+        nc.vector.tensor_reduce(page_sums[:, :G // 2], folded[:], AX.X, ALU.add)
         nc.vector.tensor_tensor(placed[:].indirect(pages[:]), page_sums[:], factor[:], ALU.mult)
         result = sb.tile([P, U], F32, name="result")
         for h in range(2):

@@ -20,12 +20,15 @@ AX = mybir.AxisListType
 
 P = 128
 PACK = 4
+LIST_ROWS = 16
 HALF = 512
 HALVES = I // HALF
 PAGE = I // G
+GRAD_SCALE = 64.0
 SOFT = 8.0
 QUADRANT = 32
-SCALE_ROWS = 16
+QUAD_BLOCKS = 4
+SCALE_ROWS = D // 32
 COPIES = QUADRANT // SCALE_ROWS
 LAST_QUADRANT = P - QUADRANT
 DEAL = I // P
@@ -40,16 +43,17 @@ def tile_attend_bpagerate_kernel(tc, query, keys_words, keys_scales, ptab, age, 
         sb = ctx.enter_context(tc.tile_pool(name="sb", bufs=1))
         ps = ctx.enter_context(tc.psum_pool(name="ps", bufs=1))
 
-        slots = lists.tile([P, I // 16], U16, name="slots")
-        pages = lists.tile([P, G // 16], U16, name="pages")
+        slots = lists.tile([P, I // LIST_ROWS], U16, name="slots")
+        pages = lists.tile([P, G // LIST_ROWS], U16, name="pages")
 
         def half_list(h):
-            return slots[:, h * (HALF // 16):(h + 1) * (HALF // 16)]
+            return slots[:, h * (HALF // LIST_ROWS):(h + 1) * (HALF // LIST_ROWS)]
 
         age_col = sb.tile([P, DEAL], F32, name="age_col")
         nc.gpsimd.dma_start(age_col[:], age[0].rearrange("(p c) -> p c", c=DEAL))
-        def scale_window(name, scales):
-            window = sb.tile([P, T], U8, name=name, tag=name)
+
+        def scale_window(tag, scales):
+            window = sb.tile([P, T], U8, name=tag, tag=tag, align_bytes=64)
             words = window[:].bitcast(I32)
             nc.vector.memset(words[:LAST_QUADRANT, :], 0)
             nc.sync.dma_start(words[LAST_QUADRANT:, :],
@@ -57,12 +61,12 @@ def tile_attend_bpagerate_kernel(tc, query, keys_words, keys_scales, ptab, age, 
             return window
 
         nc.sync.dma_start(slots[:], offs)
-        key_scales = scale_window("vals", keys_scales)
+        key_scales = scale_window("big_window", keys_scales)
         nc.sync.dma_start(pages[:], offs2)
         ptab_sb = sb.tile([P, U], F32, name="ptab_sb")
         nc.sync.dma_start(ptab_sb[:], ptab)
         val_scales = scale_window("val_scales", vals_scales)
-        query_sb = sb.tile([P, PACK, Q], F32, name="query_sb")
+        query_sb = sb.tile([P, PACK, Q], F32, name="query_sb", tag="query")
         nc.sync.dma_start(query_sb[:], query.rearrange("(p j) q -> p j q", j=PACK))
         key_words = sb.tile([P, T], U32, name="key_words")
         nc.sync.dma_start(key_words[:].bitcast(I32),
@@ -75,17 +79,24 @@ def tile_attend_bpagerate_kernel(tc, query, keys_words, keys_scales, ptab, age, 
         placed = sb.tile([P, U], F32, name="placed")
         nc.gpsimd.memset(placed[:], 0.0)
 
+        def interleave(name, raw):
+            grouped = sb.tile([P, Q, PACK], BF16, name=f"{name}_grouped", tag=f"{name}_grouped", align_bytes=64)
+            nc.scalar.copy(grouped[:], raw[:].rearrange("p j q -> p q j"))
+            return grouped
+
+        query_grouped = interleave("query", query_sb)
+
         log_rate = sb.tile([P, G], F32, name="log_rate")
         nc.vector.tensor_copy(log_rate[:], ptab_sb[:].indirect(pages[:]))
-        rate = sb.tile([P, G, P // G], F32, name="rate")
+        rate = sb.tile([P, G, P // G], F32, name="rate", tag="query")
         nc.scalar.activation(rate[:], log_rate[:].unsqueeze(2).to_broadcast([P, G, P // G]), ACT.Exp)
         rate_t = ps.tile([P, Q], F32, name="rate_t")
         nc.tensor.transpose(rate_t[:], rate[:].rearrange("q g r -> q (g r)"), ident[:])
-        fade_t = sb.tile([P, DEAL, Q], F32, name="fade_t")
+        fade_t = sb.tile([P, DEAL, Q], F32, name="fade_t", tag="gout_grouped", align_bytes=64)
         for c in range(DEAL):
             nc.scalar.activation(fade_t[:, c, :], rate_t[:], ACT.Copy, scale=age_col[:, c:c + 1])
         fade = sb.tile([P, I], F32, name="fade")
-        for b in range(HALVES):
+        for b in range(DEAL // BANK_BLOCKS):
             turned = ps.tile([P, BANK_BLOCKS, P], F32, name=f"turned{b}")
             for c in range(BANK_BLOCKS):
                 nc.tensor.transpose(turned[:, c, :], fade_t[:, b * BANK_BLOCKS + c, :], ident[:])
@@ -97,48 +108,41 @@ def tile_attend_bpagerate_kernel(tc, query, keys_words, keys_scales, ptab, age, 
             picked = sb.tile([P, I], U8, name=f"{name}_picked")
             nc.vector.tensor_copy(picked[:], window[:].indirect(slots[:]))
             plane = sb.tile([P, I], U8, name=f"{name}_plane", align_bytes=64)
-            for r in range(4):
-                nc.sync.dma_start(plane[:].bitcast(I32)[r:P:32, :],
-                                  picked[:].bitcast(I32)[LAST_QUADRANT + COPIES * r:P:4 * COPIES, :])
+            for r in range(QUAD_BLOCKS):
+                nc.sync.dma_start(plane[:].bitcast(I32)[r:P:QUADRANT, :],
+                                  picked[:].bitcast(I32)[LAST_QUADRANT + COPIES * r:P:QUAD_BLOCKS * COPIES, :])
             return plane
 
-        def gather(name, window, dtype, h, tag):
-            picked = sb.tile([P, HALF], dtype, name=f"{name}{h}", tag=tag, align_bytes=64)
+        def gather_words(name, window, h):
+            picked = sb.tile([P, HALF], U32, name=f"{name}{h}", tag=f"{name}{h}", align_bytes=64)
             nc.vector.tensor_copy(picked[:], window[:].indirect(half_list(h)))
             return picked
 
-        def interleave(name, raw):
-            grouped = sb.tile([P, Q, PACK], BF16, name=f"{name}_grouped", align_bytes=64)
-            nc.scalar.copy(grouped[:], raw[:].rearrange("p j q -> p q j"))
-            return grouped
-
-        def quantize(name, grouped):
-            codes = sb.tile([P, Q], U32, name=f"{name}_codes", align_bytes=64)
+        def quantize(name, grouped, tag):
+            codes = sb.tile([P, Q], U32, name=f"{name}_codes", tag=tag, align_bytes=64)
             scales = sb.tile([P, Q], U8, name=f"{name}_scales", align_bytes=64)
             nc.vector.quantize_mx(out=codes[:].bitcast(FP8X4), scales=scales[:],
                                   in_=grouped[:].rearrange("p q j -> p (q j)"))
             return codes, scales
 
-        def product(name, rows, words, scales, h):
+        def product(name, rows, words, plane, h):
             bank = ps.tile([P, HALF], F32, name=f"{name}{h}", tag=f"{name}{h}")
             nc.tensor.matmul_mx(out=bank[:], lhsT=rows[0][:].bitcast(FP8X4), lhsT_scale=rows[1][:],
-                                rhs=words[:].bitcast(FP8X4), rhs_scale=scales,
+                                rhs=words[:].bitcast(FP8X4), rhs_scale=plane[:, h * HALF:(h + 1) * HALF],
                                 start=True, stop=True)
             return bank
 
         key_plane = gather_plane("key", key_scales)
-        val_words = sb.tile([P, T], U32, name="val_words", tag="vals")
+        val_words = sb.tile([P, T], U32, name="val_words", tag="big_window", align_bytes=64)
         nc.sync.dma_start(val_words[:].bitcast(I32),
                           vals_words[0].rearrange("p t r -> p (t r)").bitcast(I32))
-        query_grouped = interleave("query", query_sb)
-        query_mx = quantize("query", query_grouped)
         val_plane = gather_plane("val", val_scales)
+        query_mx = quantize("query", query_grouped, "val_scales")
         gout_grouped = interleave("gout", gout_sb)
         old_sb = sb.tile([P, U], F32, name="old_sb", tag="rows")
         nc.sync.dma_start(old_sb[:], old)
-        kw = [gather("kw", key_words, U32, h, f"kw{h}") for h in range(HALVES)]
-        score = [product("score", query_mx, kw[h], key_plane[:, h * HALF:(h + 1) * HALF], h) for h in range(HALVES)]
-        gout_mx = quantize("gout", gout_grouped)
+        key_picked = [gather_words("key_picked", key_words, h) for h in range(HALVES)]
+        score = [product("score", query_mx, key_picked[h], key_plane, h) for h in range(HALVES)]
 
         logit = sb.tile([P, I], F32, name="logit")
         weight = sb.tile([P, I], F32, name="weight")
@@ -148,6 +152,7 @@ def tile_attend_bpagerate_kernel(tc, query, keys_words, keys_scales, ptab, age, 
             nc.vector.tensor_tensor(logit[:, cols], score[h][:], fade[:, cols], ALU.subtract)
             nc.scalar.activation(weight[:, cols], logit[:, cols], ACT.Exp, scale=1.0 / SOFT,
                                  accum_out=soft_sums[:, h:h + 1])
+        gout_mx = quantize("gout", gout_grouped, f"key_picked{HALVES - 1}")
         soft_sum = sb.tile([P, 1], F32, name="soft_sum")
         nc.scalar.activation(soft_sum[:], soft_sums[:, 0:1], ACT.Identity, bias=soft_sums[:, 1:2])
         shift = sb.tile([P, 1], F32, name="shift")
@@ -157,29 +162,30 @@ def tile_attend_bpagerate_kernel(tc, query, keys_words, keys_scales, ptab, age, 
         total = sb.tile([P, 1], F32, name="total")
         nc.scalar.activation(weight[:], logit[:], ACT.Exp, bias=shift[:], accum_out=total[:])
 
-        vw = [gather("vw", val_words, U32, h, f"vw{h}") for h in range(HALVES)]
-        pull = [product("pull", gout_mx, vw[h], val_plane[:, h * HALF:(h + 1) * HALF], h) for h in range(HALVES)]
+        val_picked = [gather_words("val_picked", val_words, h) for h in range(HALVES)]
+        pull = [product("pull", gout_mx, val_picked[h], val_plane, h) for h in range(HALVES)]
 
-        late = sb.tile([P, I + 1], F32, name="late", tag="vals")
+        late = sb.tile([P, I + 1], F32, name="late", tag="big_window", align_bytes=64)
         faded, inv_total = late[:, :I], late[:, I:]
         for h in range(HALVES):
             cols = slice(h * HALF, (h + 1) * HALF)
             nc.gpsimd.tensor_tensor(faded[:, cols], weight[:, cols], fade[:, cols], ALU.mult)
         terms = sb.tile([P, I], F32, name="terms")
-        means = sb.tile([P, HALVES], F32, name="means")
+        pull_sums = sb.tile([P, HALVES], F32, name="pull_sums")
         for h in range(HALVES):
             cols = slice(h * HALF, (h + 1) * HALF)
             nc.vector.scalar_tensor_tensor(logit[:, cols], pull[h][:], 1.0, weight[:, cols],
-                                           ALU.mult, ALU.mult, accum_out=means[:, h:h + 1])
+                                           ALU.mult, ALU.mult, accum_out=pull_sums[:, h:h + 1])
         mean = sb.tile([P, 1], F32, name="mean")
         nc.vector.reciprocal(inv_total, total[:])
-        nc.vector.tensor_scalar(mean[:], means[:, 0:1], means[:, 1:2], inv_total, ALU.add, ALU.mult)
+        nc.vector.tensor_scalar(mean[:], pull_sums[:, 0:1], pull_sums[:, 1:2], inv_total, ALU.add, ALU.mult)
         factor = sb.tile([P, G], F32, name="factor")
-        nc.scalar.activation(factor[:], inv_total.to_broadcast([P, G]), ACT.Copy, scale=-64.0)
+        nc.scalar.activation(factor[:], inv_total.to_broadcast([P, G]), ACT.Copy, scale=-GRAD_SCALE)
         for h in range(HALVES):
             cols = slice(h * HALF, (h + 1) * HALF)
             nc.vector.scalar_tensor_tensor(terms[:, cols], pull[h][:], mean[:], faded[:, cols],
                                            ALU.subtract, ALU.mult)
+
         page_sums = sb.tile([P, G], F32, name="page_sums")
         by_page = terms[:].rearrange("q (g r) -> q g r", r=PAGE)
         folded = sb.tile([P, G // 2, PAGE // 2], F32, name="folded")
@@ -187,8 +193,8 @@ def tile_attend_bpagerate_kernel(tc, query, keys_words, keys_scales, ptab, age, 
         nc.vector.tensor_reduce(page_sums[:, G // 2:], by_page[:, G // 2:, :], AX.X, ALU.add)
         nc.vector.tensor_reduce(page_sums[:, :G // 2], folded[:], AX.X, ALU.add)
         nc.vector.tensor_tensor(placed[:].indirect(pages[:]), page_sums[:], factor[:], ALU.mult)
+
         result = sb.tile([P, U], F32, name="result")
-        for h in range(2):
-            cols = slice(h * U // 2, (h + 1) * U // 2)
+        for cols in (slice(0, U // 2), slice(U // 2, U)):
             nc.vector.tensor_tensor(result[:, cols], placed[:, cols], old_sb[:, cols], ALU.add)
             nc.sync.dma_start(out[:, cols], result[:, cols])

import math
from contextlib import ExitStack

import concourse.mybir as mybir
from concourse.masks import make_identity

D, E, T, I, G, U, Q = 512, 512, 4096, 1024, 64, 512, 128
FLOPS = 2 * Q * I * (D + E)

F32 = mybir.dt.float32
BF16 = mybir.dt.bfloat16
I32 = mybir.dt.int32
U32 = mybir.dt.uint32
U16 = mybir.dt.uint16
U8 = mybir.dt.uint8
FP8X4 = mybir.dt.float8_e4m3fn_x4
ALU = mybir.AluOpType
ACT = mybir.ActivationFunctionType
AX = mybir.AxisListType

P = 128
PACK = 4
LIST_ROWS = 16
HALF = 512
HALVES = I // HALF
PAGE = I // G
GRAD_SCALE = 64.0
SOFT = 8.0
QUADRANT = 32
QUAD_BLOCKS = 4
SCALE_ROWS = D // 32
COPIES = QUADRANT // SCALE_ROWS
LAST_QUADRANT = P - QUADRANT
DEAL = I // P
BANK_BLOCKS = HALF // P


def tile_attend_bpagerate_kernel(tc, query, keys_words, keys_scales, ptab, age, gout,
                                  vals_words, vals_scales, old, offs, offs2, out):
    nc = tc.nc
    with ExitStack() as ctx:
        lists = ctx.enter_context(tc.tile_pool(name="lists", bufs=1))
        sb = ctx.enter_context(tc.tile_pool(name="sb", bufs=1))
        ps = ctx.enter_context(tc.psum_pool(name="ps", bufs=1))

        slots = lists.tile([P, I // LIST_ROWS], U16, name="slots")
        pages = lists.tile([P, G // LIST_ROWS], U16, name="pages")

        def half_list(h):
            return slots[:, h * (HALF // LIST_ROWS):(h + 1) * (HALF // LIST_ROWS)]

        age_col = sb.tile([P, DEAL], F32, name="age_col")
        nc.gpsimd.dma_start(age_col[:], age[0].rearrange("(p c) -> p c", c=DEAL))

        def scale_window(tag, scales):
            window = sb.tile([P, T], U8, name=tag, tag=tag, align_bytes=64)
            words = window[:].bitcast(I32)
            nc.vector.memset(words[:LAST_QUADRANT, :], 0)
            nc.sync.dma_start(words[LAST_QUADRANT:, :],
                              scales[0].bitcast(I32).unsqueeze(1).to_broadcast([SCALE_ROWS, COPIES, T // 4]))
            return window

        nc.sync.dma_start(slots[:], offs)
        key_scales = scale_window("big_window", keys_scales)
        nc.sync.dma_start(pages[:], offs2)
        ptab_sb = sb.tile([P, U], F32, name="ptab_sb")
        nc.sync.dma_start(ptab_sb[:], ptab)
        val_scales = scale_window("val_scales", vals_scales)
        query_sb = sb.tile([P, PACK, Q], F32, name="query_sb", tag="query")
        nc.sync.dma_start(query_sb[:], query.rearrange("(p j) q -> p j q", j=PACK))
        key_words = sb.tile([P, T], U32, name="key_words")
        nc.sync.dma_start(key_words[:].bitcast(I32),
                          keys_words[0].rearrange("p t r -> p (t r)").bitcast(I32))
        gout_sb = sb.tile([P, PACK, Q], F32, name="gout_sb", tag="rows")
        nc.sync.dma_start(gout_sb[:], gout.rearrange("(p j) q -> p j q", j=PACK))

        ident = sb.tile([P, P], F32, name="ident")
        make_identity(nc, ident[:])
        placed = sb.tile([P, U], F32, name="placed")
        nc.gpsimd.memset(placed[:], 0.0)

        def interleave(name, raw):
            grouped = sb.tile([P, Q, PACK], BF16, name=f"{name}_grouped", tag=f"{name}_grouped", align_bytes=64)
            nc.scalar.copy(grouped[:], raw[:].rearrange("p j q -> p q j"))
            return grouped

        query_grouped = interleave("query", query_sb)

        log_rate = sb.tile([P, G], F32, name="log_rate")
        nc.vector.tensor_copy(log_rate[:], ptab_sb[:].indirect(pages[:]))
        rate = sb.tile([P, G, P // G], F32, name="rate", tag="query")
        nc.scalar.activation(rate[:], log_rate[:].unsqueeze(2).to_broadcast([P, G, P // G]), ACT.Exp)
        rate_t = ps.tile([P, Q], F32, name="rate_t")
        nc.tensor.transpose(rate_t[:], rate[:].rearrange("q g r -> q (g r)"), ident[:])
        fade_t = sb.tile([P, DEAL, Q], F32, name="fade_t", tag="gout_grouped", align_bytes=64)
        for c in range(DEAL):
            nc.scalar.activation(fade_t[:, c, :], rate_t[:], ACT.Copy, scale=age_col[:, c:c + 1])
        fade = sb.tile([P, I], F32, name="fade")
        for b in range(DEAL // BANK_BLOCKS):
            turned = ps.tile([P, BANK_BLOCKS, P], F32, name=f"turned{b}")
            for c in range(BANK_BLOCKS):
                nc.tensor.transpose(turned[:, c, :], fade_t[:, b * BANK_BLOCKS + c, :], ident[:])
            nc.scalar.copy(
                fade[:].rearrange("q (p c) -> q p c", c=DEAL)[:, :, b * BANK_BLOCKS:(b + 1) * BANK_BLOCKS],
                turned[:].rearrange("q c p -> q p c"))

        def gather_plane(name, window):
            picked = sb.tile([P, I], U8, name=f"{name}_picked")
            nc.vector.tensor_copy(picked[:], window[:].indirect(slots[:]))
            plane = sb.tile([P, I], U8, name=f"{name}_plane", align_bytes=64)
            for r in range(QUAD_BLOCKS):
                nc.sync.dma_start(plane[:].bitcast(I32)[r:P:QUADRANT, :],
                                  picked[:].bitcast(I32)[LAST_QUADRANT + COPIES * r:P:QUAD_BLOCKS * COPIES, :])
            return plane

        def gather_words(name, window, h):
            picked = sb.tile([P, HALF], U32, name=f"{name}{h}", tag=f"{name}{h}", align_bytes=64)
            nc.vector.tensor_copy(picked[:], window[:].indirect(half_list(h)))
            return picked

        def quantize(name, grouped, tag):
            codes = sb.tile([P, Q], U32, name=f"{name}_codes", tag=tag, align_bytes=64)
            scales = sb.tile([P, Q], U8, name=f"{name}_scales", align_bytes=64)
            nc.vector.quantize_mx(out=codes[:].bitcast(FP8X4), scales=scales[:],
                                  in_=grouped[:].rearrange("p q j -> p (q j)"))
            return codes, scales

        def product(name, rows, words, plane, h):
            bank = ps.tile([P, HALF], F32, name=f"{name}{h}", tag=f"{name}{h}")
            nc.tensor.matmul_mx(out=bank[:], lhsT=rows[0][:].bitcast(FP8X4), lhsT_scale=rows[1][:],
                                rhs=words[:].bitcast(FP8X4), rhs_scale=plane[:, h * HALF:(h + 1) * HALF],
                                start=True, stop=True)
            return bank

        key_plane = gather_plane("key", key_scales)
        val_words = sb.tile([P, T], U32, name="val_words", tag="big_window", align_bytes=64)
        nc.sync.dma_start(val_words[:].bitcast(I32),
                          vals_words[0].rearrange("p t r -> p (t r)").bitcast(I32))
        val_plane = gather_plane("val", val_scales)
        query_mx = quantize("query", query_grouped, "val_scales")
        gout_grouped = interleave("gout", gout_sb)
        old_sb = sb.tile([P, U], F32, name="old_sb", tag="rows")
        nc.sync.dma_start(old_sb[:], old)
        key_picked = [gather_words("key_picked", key_words, h) for h in range(HALVES)]
        score = [product("score", query_mx, key_picked[h], key_plane, h) for h in range(HALVES)]

        logit = sb.tile([P, I], F32, name="logit")
        weight = sb.tile([P, I], F32, name="weight")
        soft_sums = sb.tile([P, HALVES], F32, name="soft_sums")
        for h in range(HALVES):
            cols = slice(h * HALF, (h + 1) * HALF)
            nc.vector.tensor_tensor(logit[:, cols], score[h][:], fade[:, cols], ALU.subtract)
            nc.scalar.activation(weight[:, cols], logit[:, cols], ACT.Exp, scale=1.0 / SOFT,
                                 accum_out=soft_sums[:, h:h + 1])
        gout_mx = quantize("gout", gout_grouped, f"key_picked{HALVES - 1}")
        soft_sum = sb.tile([P, 1], F32, name="soft_sum")
        nc.scalar.activation(soft_sum[:], soft_sums[:, 0:1], ACT.Identity, bias=soft_sums[:, 1:2])
        shift = sb.tile([P, 1], F32, name="shift")
        nc.scalar.activation(shift[:], soft_sum[:].bitcast(U32), ACT.Copy,
                             scale=-SOFT * math.log(2.0) / 2.0 ** 23,
                             bias=SOFT * (127.0 * math.log(2.0) + 0.5 * math.log(I)))
        total = sb.tile([P, 1], F32, name="total")
        nc.scalar.activation(weight[:], logit[:], ACT.Exp, bias=shift[:], accum_out=total[:])

        val_picked = [gather_words("val_picked", val_words, h) for h in range(HALVES)]
        pull = [product("pull", gout_mx, val_picked[h], val_plane, h) for h in range(HALVES)]

        late = sb.tile([P, I + 1], F32, name="late", tag="big_window", align_bytes=64)
        faded, inv_total = late[:, :I], late[:, I:]
        for h in range(HALVES):
            cols = slice(h * HALF, (h + 1) * HALF)
            nc.gpsimd.tensor_tensor(faded[:, cols], weight[:, cols], fade[:, cols], ALU.mult)
        terms = sb.tile([P, I], F32, name="terms")
        pull_sums = sb.tile([P, HALVES], F32, name="pull_sums")
        for h in range(HALVES):
            cols = slice(h * HALF, (h + 1) * HALF)
            nc.vector.scalar_tensor_tensor(logit[:, cols], pull[h][:], 1.0, weight[:, cols],
                                           ALU.mult, ALU.mult, accum_out=pull_sums[:, h:h + 1])
        mean = sb.tile([P, 1], F32, name="mean")
        nc.vector.reciprocal(inv_total, total[:])
        nc.vector.tensor_scalar(mean[:], pull_sums[:, 0:1], pull_sums[:, 1:2], inv_total, ALU.add, ALU.mult)
        factor = sb.tile([P, G], F32, name="factor")
        nc.scalar.activation(factor[:], inv_total.to_broadcast([P, G]), ACT.Copy, scale=-GRAD_SCALE)
        for h in range(HALVES):
            cols = slice(h * HALF, (h + 1) * HALF)
            nc.vector.scalar_tensor_tensor(terms[:, cols], pull[h][:], mean[:], faded[:, cols],
                                           ALU.subtract, ALU.mult)

        page_sums = sb.tile([P, G], F32, name="page_sums")
        by_page = terms[:].rearrange("q (g r) -> q g r", r=PAGE)
        folded = sb.tile([P, G // 2, PAGE // 2], F32, name="folded")
        nc.gpsimd.tensor_tensor(folded[:], by_page[:, :G // 2, :PAGE // 2], by_page[:, :G // 2, PAGE // 2:], ALU.add)
        nc.vector.tensor_reduce(page_sums[:, G // 2:], by_page[:, G // 2:, :], AX.X, ALU.add)
        nc.vector.tensor_reduce(page_sums[:, :G // 2], folded[:], AX.X, ALU.add)
        nc.vector.tensor_tensor(placed[:].indirect(pages[:]), page_sums[:], factor[:], ALU.mult)

        result = sb.tile([P, U], F32, name="result")
        for cols in (slice(0, U // 2), slice(U // 2, U)):
            nc.vector.tensor_tensor(result[:, cols], placed[:, cols], old_sb[:, cols], ALU.add)
            nc.sync.dma_start(out[:, cols], result[:, cols])
